import numpy as np, ml_dtypes
CORES = [21,29,37,45,53,61,69,77,85]
N = 9
GR, GC = 3, 3
L, KA, KB, F = 3, 1, 1, 512
def setup_inputs(rng):
    return {"a": rng.standard_normal((N, 128, KA * 128), dtype=np.float32).astype(ml_dtypes.bfloat16), "b": rng.standard_normal((N, 128, KB * F), dtype=np.float32).astype(ml_dtypes.bfloat16)}
def reference(a, b):
    A, B = a.astype(np.float64), b.astype(np.float64)
    y = np.zeros((N, 128, F))
    for i in range(GR):
        for j in range(GC):
            for k in range(L):
                At = A[i * GC + k // KA][:, 128 * (k % KA):128 * (k % KA) + 128]
                Bt = B[(k // KB) * GC + j][:, F * (k % KB):F * (k % KB) + F]
                y[i * GC + j] += At.T @ Bt
    return {"y": y.astype(ml_dtypes.bfloat16 if a.dtype != np.float64 else np.float64)}

from concourse.bass import DstId, RemoteDMATransfer

GR, GC, L, F = 3, 3, 3, 512
M = 128
H = F // 2
NA_HAND = 4
NB_HAND = 8

SCRATCH = {
    "sa": ("dram", [128, M], "bfloat16"),
    "sb": ("dram", [128, F], "bfloat16"),
    "abuf": ("sbuf", [128, L * M], "bfloat16"),
    "bbuf": ("sbuf", [128, L * F], "bfloat16"),
    "ysb": ("sbuf", [128, F], "bfloat16"),
    "ps0": ("psum", [128, F], "float32"),
    "ps1": ("psum", [128, F], "float32"),
}
SEMAPHORES = ["lsa", "lsb", "lda", "ldb", "ha", "hb", "snt", "ra0", "ra1", "ra2", "rb0", "rb1", "rb2",
              "mm0", "mm1", "cp0", "cp1", "st"]


def _bits(mask):
    return [e for e in range(mask.bit_length()) if (mask >> e) & 1]


def _mask(engines):
    m = 0
    for e in engines:
        m |= 1 << e
    return m


def _links(topo, src, dst):
    cs, cd, d = topo.chip(src), topo.chip(dst), topo.die(src)
    if cs == cd:
        return []
    if topo.mates(cs, cd):
        return [("mate", cs, d)]
    if topo.same_plane(cs, cd):
        return [("out", cs, d), ("in", cd, d)]
    m = [c for c in range(topo.CHIPS) if topo.mates(cs, c)][0]
    return [("mate", cs, d), ("out", m, d), ("in", cd, d)]


def _plan(T, topo):
    cores = list(T.cores)
    load = {}
    flows = []
    for r, rc in enumerate(cores):
        i, j = divmod(r, GC)
        chip_cores = [x for x in range(topo.CORES_PER_CHIP * topo.CHIPS)
                      if topo.chip(x) == topo.chip(rc) and x not in cores]
        free = [x for x in chip_cores if all(topo.may_write(x, d) for d in cores)]
        free.sort(key=lambda x: (topo.die(x) != topo.die(rc), x))
        bports = []
        for q in [k * GC + j for k in range(GR) if k != i]:
            if topo.may_write(rc, cores[q]):
                flows.append(("b", r, q, None))
                continue
            p = min(free, key=lambda x: (max(load.get(l, 0) for l in _links(topo, x, cores[q])), free.index(x)))
            for l in _links(topo, p, cores[q]):
                load[l] = load.get(l, 0) + 1
            free.remove(p)
            bports.append(p)
            flows.append(("b", r, q, p))
        slots = bports + free
        mates = sorted([i * GC + k for k in range(GC) if k != j], key=lambda q: topo.may_write(rc, cores[q]))
        for n, q in enumerate(mates):
            if n < len(bports) or not topo.may_write(rc, cores[q]):
                flows.append(("a", r, q, slots[n]))
            else:
                flows.append(("a", r, q, None))
    return flows


def _land(T, kind, src):
    if kind == "a":
        k = src % GC
        return T.abuf[:, k * M:(k + 1) * M], T.sem["ra%d" % k]
    k = src // GC
    return T.bbuf[:, k * F:(k + 1) * F], T.sem["rb%d" % k]


def _final(g, T, topo, core, flow):
    kind, src, dst, _ = flow
    dc = T.cores[dst]
    rid, pid, _ = topo.addr(dc)
    out, sem = _land(T, kind, src)
    mask = topo.mask(core, dc)
    g.remote_dma(out_ap=out, in_ap=(T.sa if kind == "a" else T.sb)[:], remote_sem=sem, local_sem=T.sem.snt,
                 pid=pid, routing_id=rid, dma_engine_mask=mask)
    return len(_bits(mask))


def _hand(g, T, topo, core, kind, flows):
    n = NA_HAND if kind == "a" else NB_HAND
    buf, sem = (T.sa, T.sem.ha) if kind == "a" else (T.sb, T.sem.hb)
    trs = []
    for t, f in enumerate(flows):
        rid, pid, _ = topo.addr(f[3])
        trs.append(RemoteDMATransfer(dst_ids=[DstId(rid=rid, pnc=pid)],
                                     dma_engine_mask=_mask(_bits(topo.mask(core, f[3]))[t::2][:n]),
                                     remote_sem=sem, src=buf[:], dst=buf[:]))
    g.remote_dma_fused(trs, local_sem=T.sem.snt)
    return n * len(flows)


def _port_program(g, core, T, topo, mine):
    sent = 0
    for kind, sem, n in (("a", T.sem.ha, NA_HAND), ("b", T.sem.hb, NB_HAND)):
        for f in mine:
            if f[0] == kind:
                g.wait_ge(sem, n)
                sent += _final(g, T, topo, core, f)
    g.wait_ge(T.sem.snt, sent)


def rank_program(g, core, T, topo):
    flows = _plan(T, topo)
    rank = T.rank_of(core)
    if rank is None:
        mine = [f for f in flows if f[3] == core]
        if mine:
            _port_program(g, core, T, topo, mine)
        return
    i, j = divmod(rank, GC)
    S = T.sem

    g.sync.dma_start(T.sa[:], T.a[:]).then_inc(S.lsa, 16)
    g.scalar.dma_start(T.sb[:], T.b[:]).then_inc(S.lsb, 16)
    g.sync.dma_start(T.bbuf[:, i * F:(i + 1) * F], T.b[:]).then_inc(S.ldb, 16)
    g.scalar.dma_start(T.abuf[:, j * M:(j + 1) * M], T.a[:]).then_inc(S.lda, 16)

    out = [f for f in flows if f[1] == rank]
    sent = 0
    g.wait_ge(S.lsa, 16)
    sent += _hand(g, T, topo, core, "a", [f for f in out if f[0] == "a" and f[3] is not None])
    g.wait_ge(S.lsb, 16)
    sent += _hand(g, T, topo, core, "b", [f for f in out if f[0] == "b" and f[3] is not None])
    for kind in ("b", "a"):
        for f in out:
            if f[0] == kind and f[3] is None:
                sent += _final(g, T, topo, core, f)

    def sender(f):
        return T.cores[f[1]] if f[3] is None else f[3]

    a_in = {f[1] % GC: f for f in flows if f[0] == "a" and f[2] == rank}
    b_in = {f[1] // GC: f for f in flows if f[0] == "b" and f[2] == rank}

    def when(k):
        if k == i:
            return (0, 0)
        f = b_in[k]
        return (1, 0) if f[3] is None else (2, topo.die(f[3]) != topo.die(core))

    ks = sorted(range(L), key=when)
    ps = (T.ps0, T.ps1)
    mm = (S.mm0, S.mm1)
    for n, k in enumerate(ks):
        if k == j:
            g.tensor.wait_ge(S.lda, 16)
        else:
            g.tensor.wait_ge(S["ra%d" % k], len(_bits(topo.mask(sender(a_in[k]), core))))
        if k == i:
            g.tensor.wait_ge(S.ldb, 16)
        else:
            g.tensor.wait_ge(S["rb%d" % k], len(_bits(topo.mask(sender(b_in[k]), core))))
        for h in range(2):
            ins = g.tensor.matmul(ps[h][:, 0:H], T.abuf[:, k * M:(k + 1) * M],
                                  T.bbuf[:, k * F + h * H:k * F + (h + 1) * H], n == 0, n == L - 1)
            if n == L - 1:
                ins.then_inc(mm[h], 1)

    g.vector.wait_ge(S.mm0, 1)
    g.vector.tensor_copy(T.ysb[:, 0:H], T.ps0[:, 0:H]).then_inc(S.cp0, 1)
    g.vector.wait_ge(S.mm1, 1)
    g.vector.tensor_copy(T.ysb[:, H:F], T.ps1[:, 0:H]).then_inc(S.cp1, 1)
    g.sync.wait_ge(S.cp0, 1)
    g.sync.dma_start(T.y[:, 0:H], T.ysb[:, 0:H]).then_inc(S.st, 16)
    g.scalar.wait_ge(S.cp1, 1)
    g.scalar.dma_start(T.y[:, H:F], T.ysb[:, H:F]).then_inc(S.st, 16)

    g.wait_ge(S.snt, sent)
    g.wait_ge(S.st, 32)
